import numpy as np
import ml_dtypes


def mxq(x, axis, fmt="e4m3"):
    dtype, down = {"e4m3": (ml_dtypes.float8_e4m3fn, 7), "e5m2": (ml_dtypes.float8_e5m2, 14)}[fmt]
    v = np.moveaxis(np.asarray(x, np.float32).astype(ml_dtypes.bfloat16).astype(np.float64), axis, -1)
    blocks = v.reshape(v.shape[:-1] + (-1, 32))
    amax = np.abs(blocks).max(-1, keepdims=True)
    byte = np.maximum(np.where(amax > 0, np.frexp(amax)[1] - 1 + 127, 0) - down, 1)
    scale = np.exp2(byte - 127.0)
    codes = (blocks / scale).astype(np.float32).astype(dtype).astype(np.float64)
    return np.moveaxis((codes * scale).reshape(v.shape), -1, axis)


WIDE = False


def mx_kscale(k):
    if not WIDE:
        return np.ones(k)
    levels = np.array([10, -10, 5, -5, 0])
    if k % 512:
        return np.exp2(np.random.permutation(np.resize(levels, k // 32))).repeat(32)
    a = np.empty((k // 512, 16))
    for p in range(k // 512):
        a[p, :8] = np.random.permutation(np.resize(levels, 8))
        for g in range(8):
            far = levels[np.abs(levels - a[p, g]) >= 10]
            a[p, g + 8] = far[np.random.randint(len(far))]
    return np.exp2(a.ravel()).repeat(32)


BF16 = ml_dtypes.bfloat16


def bf(x):
    return np.asarray(x, np.float32).astype(BF16)


def f64(x):
    return np.asarray(x).astype(np.float64)

E4M3FN = np.array([(-1.0 if i & 128 else 1.0) * ((1.0 + (i & 7) / 8.0) * 2.0 ** (((i >> 3) & 15) - 7) if i & 120 else (i & 7) * 2.0 ** -9) for i in range(256)])


def e4m3fn_bytes(y):
    return np.clip(np.asarray(y, np.float64), -448.0, 448.0).astype(np.float32).astype(ml_dtypes.float8_e4m3fn).view(np.uint8)


def e4m3fn_values(b):
    return E4M3FN[b]


T, H, D, S = 512, 8, 512, 2048


def setup_inputs():
    s = mx_kscale(D)
    q = np.random.standard_normal((T, H, D)) / np.sqrt(D) * s
    k = np.random.standard_normal((S, D)) / s[None, :]
    k_scale = (np.max(np.abs(k), axis=1, keepdims=True) / 448.0).astype(np.float32)
    k_bytes = e4m3fn_bytes(k / k_scale.astype(np.float64))
    w = (0.1 + np.abs(np.random.standard_normal((T, H)))) / np.sqrt(H)
    return {"q": bf(q),
            "k_bytes": k_bytes,
            "k_scale": k_scale,
            "w": bf(w)}


def reference(q, k_bytes, k_scale, w):
    k = e4m3fn_values(k_bytes) * np.repeat(f64(k_scale), D, axis=1)
    qq = mxq(f64(q), 2, "e4m3")
    kq = mxq(k, 1, "e4m3")
    dots = qq.reshape(T * H, D) @ kq.T
    act = np.maximum(dots, 0.0).reshape(T, H, S)
    weighted = act * f64(w)[:, :, None]
    return np.sum(weighted, axis=1)

@@ -1,0 +1,312 @@
+from contextlib import ExitStack
+
+import concourse.mybir as mybir
+from concourse.masks import make_identity
+
+F32 = mybir.dt.float32
+BF16 = mybir.dt.bfloat16
+U32 = mybir.dt.uint32
+U8 = mybir.dt.uint8
+FP8 = mybir.dt.float8_e4m3fn
+FP8X4 = mybir.dt.float8_e4m3fn_x4
+ACT = mybir.ActivationFunctionType
+ALU = mybir.AluOpType
+
+P = 128
+T, H, D, S = 512, 8, 512, 2048
+NT = T // P
+SC = 512
+NC = S // SC
+
+FLOPS = 2 * T * H * D * S + 3 * T * H * S
+
+TINY = 1e-20
+
+
+def tile_sparse_indexer_scores_d3_kernel(tc, q, k_bytes, k_scale, w, out):
+    nc = tc.nc
+    with ExitStack() as ctx:
+        keep = ctx.enter_context(tc.tile_pool(name="keep", bufs=1))
+        work = ctx.enter_context(tc.tile_pool(name="work", bufs=3))
+        ps_t = ctx.enter_context(tc.psum_pool(name="ps_t", bufs=2))
+        ps_a = ctx.enter_context(tc.psum_pool(name="ps_a", bufs=3))
+        ps_d = ctx.enter_context(tc.psum_pool(name="ps_d", bufs=3))
+
+        q_v = q.rearrange("(p i) h d -> i p h d", i=NT)
+        kb_v = k_bytes.rearrange("(c p j) d -> c p (j d)", p=P, j=4)
+        ks_v = k_scale.rearrange("(c p j) o -> p c (j o)", p=P, j=4)
+        w_v = w.rearrange("(p i) h -> p (i h)", i=NT)
+        out_v = out.rearrange("(p i) s -> i p s", i=NT)
+
+        ks = keep.tile([P, NC, 4], F32, name="ks")
+        wb = keep.tile([P, NT * H], BF16, name="wb")
+        kb = [keep.tile([P, 4, D], U8, name=f"kb{c}") for c in range(NC)]
+        qr0 = [keep.tile([P, 2, D], BF16, name=f"qr0_{p}") for p in range(4)]
+        qr = [None] + [keep.tile([P, H, D], BF16, name=f"qr{i}") for i in range(1, NT)]
+
+        def load_k(c):
+            nc.sync.dma_start(out=kb[c][:].rearrange("p j d -> p (j d)"), in_=kb_v[c])
+
+        def load_q0(p):
+            nc.sync.dma_start(out=qr0[p][:], in_=q_v[0][:, 2 * p : 2 * p + 2, :])
+
+        load_k(0)
+        nc.sync.dma_start(out=ks[:], in_=ks_v)
+        load_q0(0)
+        load_k(1)
+        load_q0(1)
+        nc.sync.dma_start(out=wb[:], in_=w_v)
+        load_q0(2)
+        load_q0(3)
+        nc.sync.dma_start(out=qr[1][:], in_=q_v[1])
+        load_k(2)
+        nc.sync.dma_start(out=qr[2][:], in_=q_v[2])
+        load_k(3)
+        nc.sync.dma_start(out=qr[3][:], in_=q_v[3])
+
+        ident = keep.tile([P, P], F32, name="ident")
+        make_identity(nc, ident[:])
+        warm = keep.tile([P, 1], F32, name="warm")
+        nc.vector.memset(warm[:], 0.0)
+        warm2 = keep.tile([P, 1], F32, name="warm2")
+        nc.scalar.activation(out=warm2[:], in_=warm[:], func=ACT.Relu)
+
+        kg = [keep.tile([P, SC, 4], BF16, name=f"kg{c}", align_bytes=64) for c in range(NC)]
+        kw = [keep.tile([P, 4, D], BF16, name=f"kw{c}", align_bytes=64) for c in range(NC)]
+        kc = keep.tile([P, S], U32, name="kc", align_bytes=64)
+        ksc = keep.tile([P, S], U8, name="ksc", align_bytes=64)
+        qg = [keep.tile([P, H * P, 4], BF16, name=f"qg{i}", align_bytes=64) for i in range(NT)]
+        qc = [keep.tile([P, H * P], U32, name=f"qc{i}", align_bytes=64) for i in range(NT)]
+        qsc = [keep.tile([P, H * P], U8, name=f"qsc{i}", align_bytes=64) for i in range(NT)]
+
+        def k_widen(c, j, on_act):
+            src = kb[c][:, j, :].bitcast(FP8)
+            sc = ks[:, c, j : j + 1]
+            if on_act:
+                nc.scalar.activation(out=kw[c][:, j, :], in_=src, func=ACT.Copy, scale=sc)
+            else:
+                nc.vector.tensor_scalar(out=kw[c][:, j, :], in0=src, scalar1=sc, scalar2=None, op0=ALU.mult)
+
+        def k_turn(c, pair, pool=ps_t, tag="xt"):
+            xt = pool.tile([P, 4, P], F32, name=tag, tag=tag)
+            for jj in range(2):
+                words = kw[c][:, 2 * pair + jj, :].bitcast(F32)
+                for u in range(2):
+                    nc.tensor.transpose(xt[:, 2 * jj + u, :], words[:, u::2], ident[:])
+            return xt
+
+        def k_out(c, pair, xt, on_act):
+            dst = kg[c][:].rearrange("p n e -> p (n e)").bitcast(F32).rearrange("p (r x) -> p r x", x=8)
+            dst = dst[:, :, 4 * pair : 4 * pair + 4]
+            src = xt[:].rearrange("p x r -> p r x")
+            if on_act:
+                nc.scalar.copy(out=dst, in_=src)
+            else:
+                nc.vector.tensor_copy(out=dst, in_=src)
+
+        def k_quant(c):
+            cols = slice(c * SC, (c + 1) * SC)
+            nc.vector.quantize_mx(
+                out=kc[:, cols].bitcast(FP8X4), scales=ksc[:, cols], in_=kg[c][:].rearrange("p n e -> p (n e)")
+            )
+
+        def q_turn(i, p, pool=ps_t, tag="xt"):
+            xt = pool.tile([P, 4, P], F32, name=tag, tag=tag)
+            for hh in range(2):
+                raw = qr0[p][:, hh, :] if i == 0 else qr[i][:, 2 * p + hh, :]
+                words = raw.bitcast(F32)
+                for u in range(2):
+                    nc.tensor.transpose(xt[:, 2 * hh + u, :], words[:, u::2], ident[:])
+            return xt
+
+        def q_out(i, p, xt, on_act):
+            dst = qg[i][:, 256 * p : 256 * p + 256, :].rearrange("p n e -> p (n e)").bitcast(F32)
+            dst = dst.rearrange("p (h r u) -> p h r u", h=2, u=2)
+            src = xt[:].rearrange("p (h u) r -> p h r u", u=2)
+            if on_act:
+                nc.scalar.copy(out=dst, in_=src)
+            else:
+                nc.vector.tensor_copy(out=dst, in_=src)
+
+        def q_quant(i, p):
+            cols = slice(256 * p, 256 * p + 256)
+            nc.vector.quantize_mx(
+                out=qc[i][:, cols].bitcast(FP8X4),
+                scales=qsc[i][:, cols],
+                in_=qg[i][:, cols, :].rearrange("p n e -> p (n e)"),
+            )
+
+        wf = keep.tile([P, NT, H], F32, name="wf")
+        wc = keep.tile([P, NT, H], F32, name="wc")
+        rc = keep.tile([P, NT, H], F32, name="rc")
+        ra = keep.tile([P, NT, 3], F32, name="ra")
+        rz = keep.tile([P, NT, 1], F32, name="rz")
+
+        def mx(i, c, h, pool, tag):
+            ps = pool.tile([P, SC], F32, name=tag, tag=tag)
+            qs = slice(h * P, (h + 1) * P)
+            cs = slice(c * SC, (c + 1) * SC)
+            nc.tensor.matmul_mx(
+                out=ps[:],
+                lhsT=qc[i][:, qs].bitcast(FP8X4),
+                lhsT_scale=qsc[i][:, qs],
+                rhs=kc[:, cs].bitcast(FP8X4),
+                rhs_scale=ksc[:, cs],
+                start=True,
+                stop=True,
+            )
+            return ps
+
+        def relu_scaled(ps, col, tag):
+            a = work.tile([P, SC], F32, name=tag, tag=tag)
+            nc.scalar.activation(out=a[:], in_=ps[:], func=ACT.Relu, scale=col)
+            return a
+
+        def relu_add(ps, a, tag):
+            z = work.tile([P, SC], F32, name=tag, tag=tag)
+            nc.vector.scalar_tensor_tensor(out=z[:], in0=ps[:], scalar=0.0, in1=a[:], op0=ALU.max, op1=ALU.add)
+            return z
+
+        def mul_add(z, col, y, tag):
+            o = work.tile([P, SC], F32, name=tag, tag=tag)
+            nc.vector.scalar_tensor_tensor(out=o[:], in0=z[:], scalar=col, in1=y[:], op0=ALU.mult, op1=ALU.add)
+            return o
+
+        def pair_sum(i, c, tag):
+            ps6 = mx(i, c, 6, ps_a, "pa")
+            ps7 = mx(i, c, 7, ps_a, "pa")
+            a6 = relu_scaled(ps6, wf[:, i, 6:7], "a6")
+            a7 = relu_scaled(ps7, wf[:, i, 7:8], "a7")
+            v = keep.tile([P, SC], F32, name=tag, tag=tag)
+            nc.gpsimd.tensor_tensor(out=v[:], in0=a6[:], in1=a7[:], op=ALU.add)
+            return v
+
+        units = [(0, 0), (0, 1), (1, 0), (1, 1), (0, 2), (1, 2), (2, 0), (2, 1), (2, 2), (0, 3), (1, 3), (2, 3), (3, 0), (3, 1), (3, 2), (3, 3)]
+        state = {}
+
+        def sum1(n):
+            st = state[n]
+            st["s1"] = mul_add(st["z1"], rz[:, units[n][0], 0:1], st["z3"], "s1")
+
+        def sum2(n):
+            st = state[n]
+            st["s2"] = mul_add(st["z5"], wc[:, units[n][0], 5:6], st["v"], "s2")
+
+        def sum3(n):
+            i, c = units[n]
+            st = state[n]
+            o = mul_add(st["s1"], wc[:, i, 3:4], st["s2"], "o")
+            nc.sync.dma_start(out=out_v[i][:, c * SC : (c + 1) * SC], in_=o[:])
+
+        k_widen(0, 0, False)
+        k_widen(0, 1, True)
+        k_widen(0, 2, False)
+        k_widen(0, 3, True)
+        xk0 = k_turn(0, 0)
+        xk1 = k_turn(0, 1)
+        xq = [q_turn(0, 0, ps_a, "pa"), q_turn(0, 1, ps_a, "pa"), q_turn(0, 2, ps_a, "pa"), q_turn(0, 3, ps_d, "pd")]
+        k_out(0, 0, xk0, True)
+        for j in range(4):
+            k_widen(1, j, False)
+        k_out(0, 1, xk1, True)
+        nc.vector.tensor_copy(out=wf[:].rearrange("p i h -> p (i h)"), in_=wb[:])
+        k_quant(0)
+        q_out(0, 0, xq[0], True)
+        nc.vector.tensor_scalar(out=wc[:], in0=wf[:], scalar1=TINY, scalar2=None, op0=ALU.max)
+        q_quant(0, 0)
+        nc.vector.reciprocal(out=rc[:], in_=wc[:])
+        q_out(0, 1, xq[1], True)
+        nc.vector.tensor_tensor(out=ra[:], in0=wf[:, :, 0:6:2], in1=rc[:, :, 1:6:2], op=ALU.mult)
+        q_quant(0, 1)
+        nc.vector.tensor_tensor(out=rz[:], in0=wc[:, :, 1:2], in1=rc[:, :, 3:4], op=ALU.mult)
+        q_out(0, 2, xq[2], True)
+        q_out(0, 3, xq[3], True)
+        q_quant(0, 2)
+        q_quant(0, 3)
+
+        def turn(pc):
+            return k_turn(pc[1], pc[2]) if pc[0] == "k" else q_turn(pc[1], pc[2])
+
+        def copy(pc, xt, on_act):
+            if pc[0] == "k":
+                k_out(pc[1], pc[2], xt, on_act)
+            else:
+                q_out(pc[1], pc[2], xt, on_act)
+
+        def quant(pc):
+            if pc[0] == "q":
+                q_quant(pc[1], pc[2])
+            elif pc[2] == 1:
+                k_quant(pc[1])
+
+        pieces = {
+            0: [("k", 1, 0), ("k", 1, 1)],
+            1: [("q", 1, 0), ("q", 1, 1), ("q", 1, 2), ("q", 1, 3)],
+            2: [("k", 2, 0)],
+            3: [("k", 2, 1)],
+            4: [("q", 2, 0), ("q", 2, 1)],
+            5: [("q", 2, 2), ("q", 2, 3)],
+            6: [("k", 3, 0)],
+            7: [("k", 3, 1)],
+            8: [("q", 3, 0)],
+            9: [("q", 3, 1)],
+            10: [("q", 3, 2)],
+            11: [("q", 3, 3)],
+        }
+        widen = {0: 2, 4: 3}
+        for n, (i, c) in enumerate(units):
+            st = {}
+            state[n] = st
+            pcs = pieces.get(n, [])
+            xts = {}
+
+            def early(k):
+                if k < len(pcs):
+                    xts[k] = turn(pcs[k])
+
+            def out(k, on_act=True):
+                if k < len(pcs):
+                    copy(pcs[k], xts[k], on_act)
+
+            final = n == len(units) - 1
+            if final:
+                st["v"] = pair_sum(i, c, "v2")
+            ps0 = mx(i, c, 0, ps_a, "pa")
+            ps1 = mx(i, c, 1, ps_d, "pd")
+            early(0)
+            a0 = relu_scaled(ps0, ra[:, i, 0:1], "a0")
+            st["z1"] = relu_add(ps1, a0, "z1")
+            ps2 = mx(i, c, 2, ps_a, "pa")
+            ps3 = mx(i, c, 3, ps_d, "pd")
+            early(1)
+            out(0)
+            a2 = relu_scaled(ps2, ra[:, i, 1:2], "a2")
+            st["z3"] = relu_add(ps3, a2, "z3")
+            ps4 = mx(i, c, 4, ps_a, "pa")
+            ps5 = mx(i, c, 5, ps_d, "pd")
+            early(2)
+            out(1)
+            a4 = relu_scaled(ps4, ra[:, i, 2:3], "a4")
+            st["z5"] = relu_add(ps5, a4, "z5")
+            early(3)
+            out(2)
+            if not final:
+                st["v"] = pair_sum(i, c, "v")
+            out(3)
+            if n > 1:
+                sum3(n - 2)
+            for pc in pcs[:2]:
+                quant(pc)
+            if n in widen:
+                for j in range(4):
+                    k_widen(widen[n], j, widen[n] == 3)
+            if n:
+                sum1(n - 1)
+                sum2(n - 1)
+            for pc in pcs[2:]:
+                quant(pc)
+        last = len(units) - 1
+        sum3(last - 1)
+        sum1(last)
+        sum2(last)
+        sum3(last)

@@ -21,6 +21,25 @@ NC = S // SC
 FLOPS = 2 * T * H * D * S + 3 * T * H * S
 
 TINY = 1e-20
+UNITS = [(0, 0), (0, 1), (1, 0), (1, 1), (0, 2), (1, 2), (2, 0), (2, 1), (2, 2), (0, 3), (1, 3), (2, 3), (3, 0), (3, 1), (3, 2), (3, 3)]
+LOADS = "k0 ks q0.0 q0.1 k1 wb q0.2 q0.3 q1 k2 q2 k3 q3"
+PROGRAM = ["W0.0 w0.1 W0.2 w0.3 Tk0a Tk0b Tq0.0/a Tq0.1/a W1.0 W1.1 Ck0a W1.2 W1.3 Ck0b P0 Qk0 Cq0.0 P1 Tk1a Tk1b Tq0.2/a Tq0.3/d Qq0.0 P2 Cq0.1 P3 Qq0.1 P4 Ck1a Dk1b Cq0.2 Qk1 Qq0.2 Cq0.3 Qq0.3",
+    "M0 M1 A0 A1 V M2 M3 Tq1.0 A2 F3 M4 M5 A4 F5 Tq1.1 M6 M7 Cq1.0 A6 F7 Cq1.1 Tq1.2 Tq1.3 W2.0 W2.1 W2.2 W2.3 S1 Qq1.0 Qq1.1 S2",
+    "M0 M1 A0 A1 V M2 M3 A2 F3 Cq1.2 M4 M5 A4 F5 Qq1.2 Cq1.3 M6 M7 A6 F7 Tk2a Tk2b S3- S1 Qq1.3 S2",
+    "M0 M1 A0 A1 V M2 M3 Ck2a A2 F3 M4 M5 Ck2b A4 F5 M6 M7 A6 F7 Tq2.0 Tq2.1 S3- S1 Qk2  S2",
+    "M0 M1 A0 A1 V M2 M3 Cq2.0 A2 F3 M4 M5 Cq2.1 A4 F5 M6 M7 A6 F7 Tq2.2 Tq2.3 S3- S1 Qq2.0 Qq2.1 W3.0 W3.1 S2",
+    "M0 M1 A0 A1 V M2 M3 Cq2.2 A2 F3 M4 M5 Cq2.3 A4 F5 M6 M7 A6 F7 Tk3a S3- S1 Qq2.2 Qq2.3 W3.2 W3.3 S2",
+    "M0 M1 A0 A1 V M2 M3 Ck3a A2 F3 M4 M5  A4 F5 M6 M7 A6 F7 Tk3b S3- S1   S2",
+    "M0 M1 A0 A1 V M2 M3 Ck3b A2 F3 M4 M5  A4 F5 M6 M7 A6 F7 Tq3.0 S3- S1 Qk3  S2",
+    "M0 M1 A0 A1 V M2 M3 Cq3.0 A2 F3 M4 M5  A4 F5 M6 M7 A6 F7 Tq3.1 S3- S1 Qq3.0  S2",
+    "M0 M1 A0 A1 V M2 M3 Cq3.1 A2 F3 M4 M5  A4 F5 M6 M7 A6 F7 Tq3.2 S3- S1 Qq3.1  S2",
+    "M0 M1 A0 A1 V M2 M3 Cq3.2 A2 F3 M4 M5  A4 F5 M6 M7 A6 F7 Tq3.3 S3- S1 Qq3.2  S2",
+    "M0 M1 A0 A1 V M2 M3 Cq3.3 A2 F3 M4 M5  A4 F5 M6 M7 A6 F7  S3- S1 Qq3.3  S2",
+    "M0 M1 A0 A1 V M2 M3  A2 F3 M4 M5  A4 F5 M6 M7 A6 F7  S3- S1   S2",
+    "M0 M1 A0 A1 V M2 M3  A2 F3 M4 M5  A4 F5 M6 M7 A6 F7  S3- S1   S2",
+    "M0 M1 A0 A1 V M2 M3  A2 F3 M4 M5  A4 F5 M6 M7 A6 F7  S3- S1   S2",
+    "M0 M1 A0 A1 V M2 M3  A2 F3 M4 M5  A4 F5 M6 M7 A6 F7  S3- S1   S2",
+    "M0 M1 A0 A1 V M2 M3  A2 F3 M4 M5  A4 F5 M6 M7 A6 F7  S3- S1   S2 S3"]
 
 
 def tile_sparse_indexer_scores_d3_kernel(tc, q, k_bytes, k_scale, w, out):
@@ -31,6 +50,8 @@ def tile_sparse_indexer_scores_d3_kernel(tc, q, k_bytes, k_scale, w, out):
         ps_t = ctx.enter_context(tc.psum_pool(name="ps_t", bufs=2))
         ps_a = ctx.enter_context(tc.psum_pool(name="ps_a", bufs=3))
         ps_d = ctx.enter_context(tc.psum_pool(name="ps_d", bufs=3))
+
+        ctx.enter_context(tc.manual_schedule())
 
         q_v = q.rearrange("(p i) h d -> i p h d", i=NT)
         kb_v = k_bytes.rearrange("(c p j) d -> c p (j d)", p=P, j=4)
@@ -50,19 +71,17 @@ def tile_sparse_indexer_scores_d3_kernel(tc, q, k_bytes, k_scale, w, out):
         def load_q0(p):
             nc.sync.dma_start(out=qr0[p][:], in_=q_v[0][:, 2 * p : 2 * p + 2, :])
 
-        load_k(0)
-        nc.sync.dma_start(out=ks[:], in_=ks_v)
-        load_q0(0)
-        load_k(1)
-        load_q0(1)
-        nc.sync.dma_start(out=wb[:], in_=w_v)
-        load_q0(2)
-        load_q0(3)
-        nc.sync.dma_start(out=qr[1][:], in_=q_v[1])
-        load_k(2)
-        nc.sync.dma_start(out=qr[2][:], in_=q_v[2])
-        load_k(3)
-        nc.sync.dma_start(out=qr[3][:], in_=q_v[3])
+        for tok in LOADS.split():
+            if tok == "ks":
+                nc.sync.dma_start(out=ks[:], in_=ks_v)
+            elif tok == "wb":
+                nc.sync.dma_start(out=wb[:], in_=w_v)
+            elif tok[0] == "k":
+                load_k(int(tok[1:]))
+            elif tok[:3] == "q0.":
+                load_q0(int(tok[3:]))
+            else:
+                nc.sync.dma_start(out=qr[int(tok[1:])][:], in_=q_v[int(tok[1:])])
 
         ident = keep.tile([P, P], F32, name="ident")
         make_identity(nc, ident[:])
@@ -172,141 +191,68 @@ def tile_sparse_indexer_scores_d3_kernel(tc, q, k_bytes, k_scale, w, out):
             nc.vector.scalar_tensor_tensor(out=o[:], in0=z[:], scalar=col, in1=y[:], op0=ALU.mult, op1=ALU.add)
             return o
 
-        def pair_sum(i, c, tag):
-            ps6 = mx(i, c, 6, ps_a, "pa")
-            ps7 = mx(i, c, 7, ps_a, "pa")
-            a6 = relu_scaled(ps6, wf[:, i, 6:7], "a6")
-            a7 = relu_scaled(ps7, wf[:, i, 7:8], "a7")
-            v = keep.tile([P, SC], F32, name=tag, tag=tag)
-            nc.gpsimd.tensor_tensor(out=v[:], in0=a6[:], in1=a7[:], op=ALU.add)
-            return v
+        units = UNITS
+        PS = {"x": (ps_t, "xt"), "a": (ps_a, "pa"), "d": (ps_d, "pd")}
+        R_ = {}
 
-        units = [(0, 0), (0, 1), (1, 0), (1, 1), (0, 2), (1, 2), (2, 0), (2, 1), (2, 2), (0, 3), (1, 3), (2, 3), (3, 0), (3, 1), (3, 2), (3, 3)]
-        state = {}
+        def kq(tok):
+            if tok[0] == "k":
+                return k_turn, k_out, int(tok[1]), "ab".index(tok[2])
+            return q_turn, q_out, int(tok[1]), int(tok[3])
 
-        def sum1(n):
-            st = state[n]
-            st["s1"] = mul_add(st["z1"], rz[:, units[n][0], 0:1], st["z3"], "s1")
-
-        def sum2(n):
-            st = state[n]
-            st["s2"] = mul_add(st["z5"], wc[:, units[n][0], 5:6], st["v"], "s2")
-
-        def sum3(n):
-            i, c = units[n]
-            st = state[n]
-            o = mul_add(st["s1"], wc[:, i, 3:4], st["s2"], "o")
-            nc.sync.dma_start(out=out_v[i][:, c * SC : (c + 1) * SC], in_=o[:])
-
-        k_widen(0, 0, False)
-        k_widen(0, 1, True)
-        k_widen(0, 2, False)
-        k_widen(0, 3, True)
-        xk0 = k_turn(0, 0)
-        xk1 = k_turn(0, 1)
-        xq = [q_turn(0, 0, ps_a, "pa"), q_turn(0, 1, ps_a, "pa"), q_turn(0, 2, ps_a, "pa"), q_turn(0, 3, ps_d, "pd")]
-        k_out(0, 0, xk0, True)
-        for j in range(4):
-            k_widen(1, j, False)
-        k_out(0, 1, xk1, True)
-        nc.vector.tensor_copy(out=wf[:].rearrange("p i h -> p (i h)"), in_=wb[:])
-        k_quant(0)
-        q_out(0, 0, xq[0], True)
-        nc.vector.tensor_scalar(out=wc[:], in0=wf[:], scalar1=TINY, scalar2=None, op0=ALU.max)
-        q_quant(0, 0)
-        nc.vector.reciprocal(out=rc[:], in_=wc[:])
-        q_out(0, 1, xq[1], True)
-        nc.vector.tensor_tensor(out=ra[:], in0=wf[:, :, 0:6:2], in1=rc[:, :, 1:6:2], op=ALU.mult)
-        q_quant(0, 1)
-        nc.vector.tensor_tensor(out=rz[:], in0=wc[:, :, 1:2], in1=rc[:, :, 3:4], op=ALU.mult)
-        q_out(0, 2, xq[2], True)
-        q_out(0, 3, xq[3], True)
-        q_quant(0, 2)
-        q_quant(0, 3)
-
-        def turn(pc):
-            return k_turn(pc[1], pc[2]) if pc[0] == "k" else q_turn(pc[1], pc[2])
-
-        def copy(pc, xt, on_act):
-            if pc[0] == "k":
-                k_out(pc[1], pc[2], xt, on_act)
-            else:
-                q_out(pc[1], pc[2], xt, on_act)
-
-        def quant(pc):
-            if pc[0] == "q":
-                q_quant(pc[1], pc[2])
-            elif pc[2] == 1:
-                k_quant(pc[1])
-
-        pieces = {
-            0: [("k", 1, 0), ("k", 1, 1)],
-            1: [("q", 1, 0), ("q", 1, 1), ("q", 1, 2), ("q", 1, 3)],
-            2: [("k", 2, 0)],
-            3: [("k", 2, 1)],
-            4: [("q", 2, 0), ("q", 2, 1)],
-            5: [("q", 2, 2), ("q", 2, 3)],
-            6: [("k", 3, 0)],
-            7: [("k", 3, 1)],
-            8: [("q", 3, 0)],
-            9: [("q", 3, 1)],
-            10: [("q", 3, 2)],
-            11: [("q", 3, 3)],
-        }
-        widen = {0: 2, 4: 3}
-        for n, (i, c) in enumerate(units):
-            st = {}
-            state[n] = st
-            pcs = pieces.get(n, [])
-            xts = {}
-
-            def early(k):
-                if k < len(pcs):
-                    xts[k] = turn(pcs[k])
-
-            def out(k, on_act=True):
-                if k < len(pcs):
-                    copy(pcs[k], xts[k], on_act)
-
-            final = n == len(units) - 1
-            if final:
-                st["v"] = pair_sum(i, c, "v2")
-            ps0 = mx(i, c, 0, ps_a, "pa")
-            ps1 = mx(i, c, 1, ps_d, "pd")
-            early(0)
-            a0 = relu_scaled(ps0, ra[:, i, 0:1], "a0")
-            st["z1"] = relu_add(ps1, a0, "z1")
-            ps2 = mx(i, c, 2, ps_a, "pa")
-            ps3 = mx(i, c, 3, ps_d, "pd")
-            early(1)
-            out(0)
-            a2 = relu_scaled(ps2, ra[:, i, 1:2], "a2")
-            st["z3"] = relu_add(ps3, a2, "z3")
-            ps4 = mx(i, c, 4, ps_a, "pa")
-            ps5 = mx(i, c, 5, ps_d, "pd")
-            early(2)
-            out(1)
-            a4 = relu_scaled(ps4, ra[:, i, 2:3], "a4")
-            st["z5"] = relu_add(ps5, a4, "z5")
-            early(3)
-            out(2)
-            if not final:
-                st["v"] = pair_sum(i, c, "v")
-            out(3)
-            if n > 1:
-                sum3(n - 2)
-            for pc in pcs[:2]:
-                quant(pc)
-            if n in widen:
-                for j in range(4):
-                    k_widen(widen[n], j, widen[n] == 3)
-            if n:
-                sum1(n - 1)
-                sum2(n - 1)
-            for pc in pcs[2:]:
-                quant(pc)
-        last = len(units) - 1
-        sum3(last - 1)
-        sum1(last)
-        sum2(last)
-        sum3(last)
+        for n, text in enumerate(PROGRAM):
+            u = n - 1
+            for tok in text.split():
+                op, arg = tok[0], tok[1:]
+                if op in "Ww":
+                    k_widen(int(arg[0]), int(arg[2]), op == "w")
+                elif op == "T":
+                    bank = "x"
+                    if arg[-1] in "xad" and arg[-2] == "/":
+                        bank = arg[-1]
+                        arg = arg[:-2]
+                    f, g, a, b = kq(arg)
+                    R_[arg] = f(a, b, PS[bank][0], PS[bank][1])
+                elif op in "CD":
+                    f, g, a, b = kq(arg)
+                    g(a, b, R_[arg], op == "C")
+                elif op == "Q":
+                    if arg[0] == "k":
+                        k_quant(int(arg[1]))
+                    else:
+                        q_quant(int(arg[1]), int(arg[3]))
+                elif op == "P":
+                    if arg == "0":
+                        nc.vector.tensor_copy(out=wf[:].rearrange("p i h -> p (i h)"), in_=wb[:])
+                    elif arg == "1":
+                        nc.vector.tensor_scalar(out=wc[:], in0=wf[:], scalar1=TINY, scalar2=None, op0=ALU.max)
+                    elif arg == "2":
+                        nc.vector.reciprocal(out=rc[:], in_=wc[:])
+                    elif arg == "3":
+                        nc.vector.tensor_tensor(out=ra[:], in0=wf[:, :, 2:8:2], in1=rc[:, :, 3:8:2], op=ALU.mult)
+                    else:
+                        nc.vector.tensor_tensor(out=rz[:], in0=wc[:, :, 3:4], in1=rc[:, :, 5:6], op=ALU.mult)
+                else:
+                    hs = arg.replace("-", "")
+                    v = u - (len(arg) - len(hs))
+                    h = int(hs) if hs else 0
+                    i, c = units[v]
+                    if op == "M":
+                        bank = "d" if h in (3, 5, 7) else "a"
+                        R_[("m", v, h)] = mx(i, c, h, PS[bank][0], PS[bank][1])
+                    elif op == "A":
+                        col = ra[:, i, h // 2 - 1 : h // 2] if h > 1 else wf[:, i, h : h + 1]
+                        R_[("a", v, h)] = relu_scaled(R_[("m", v, h)], col, "a%d" % h)
+                    elif op == "F":
+                        R_[("z", v, h)] = relu_add(R_[("m", v, h)], R_[("a", v, h - 1)], "z%d" % h)
+                    elif op == "V":
+                        vt = keep.tile([P, SC], F32, name="v", tag="v")
+                        nc.gpsimd.tensor_tensor(out=vt[:], in0=R_[("a", v, 0)][:], in1=R_[("a", v, 1)][:], op=ALU.add)
+                        R_[("v", v)] = vt
+                    elif op == "S" and h == 1:
+                        R_[("s1", v)] = mul_add(R_[("z", v, 3)], rz[:, i, 0:1], R_[("z", v, 5)], "s1")
+                    elif op == "S" and h == 2:
+                        R_[("s2", v)] = mul_add(R_[("z", v, 7)], wc[:, i, 7:8], R_[("v", v)], "s2")
+                    elif op == "S" and h == 3:
+                        o = mul_add(R_[("s1", v)], wc[:, i, 5:6], R_[("s2", v)], "o")
+                        nc.sync.dma_start(out=out_v[i][:, c * SC : (c + 1) * SC], in_=o[:])

@@ -14,32 +14,36 @@ ALU = mybir.AluOpType
 
 P = 128
 T, H, D, S = 512, 8, 512, 2048
-NT = T // P
+TILES = T // P
 SC = 512
-NC = S // SC
+CHUNKS = S // SC
 
 FLOPS = 2 * T * H * D * S + 3 * T * H * S
 
-TINY = 1e-20
-UNITS = [(0, 0), (0, 1), (1, 0), (1, 1), (0, 2), (1, 2), (2, 0), (2, 1), (2, 2), (0, 3), (1, 3), (2, 3), (3, 0), (3, 1), (3, 2), (3, 3)]
-LOADS = "k0 ks q0.0 q0.1 k1 wb q0.2 q0.3 q1 k2 q2 k3 q3"
-PROGRAM = ["W0.0 w0.1 W0.2 w0.3 Tk0a Tk0b Tq0.0/a Tq0.1/a W1.0 W1.1 Ck0a W1.2 W1.3 Ck0b P0 Qk0 Cq0.0 P1 Tk1a Tk1b Tq0.2/a Tq0.3/d Qq0.0 P2 Cq0.1 P3 Qq0.1 P4 Ck1a Dk1b Cq0.2 Qk1 Qq0.2 Cq0.3 Qq0.3",
-    "M0 M1 A0 A1 V M2 M3 Tq1.0 A2 F3 M4 M5 A4 F5 Tq1.1 M6 M7 Cq1.0 A6 F7 Cq1.1 Tq1.2 Tq1.3 W2.0 W2.1 W2.2 W2.3 S1 Qq1.0 Qq1.1 S2",
-    "M0 M1 A0 A1 V M2 M3 A2 F3 Cq1.2 M4 M5 A4 F5 Qq1.2 Cq1.3 M6 M7 A6 F7 Tk2a Tk2b S3- S1 Qq1.3 S2",
-    "M0 M1 A0 A1 V M2 M3 Ck2a A2 F3 M4 M5 Ck2b A4 F5 M6 M7 A6 F7 Tq2.0 Tq2.1 S3- S1 Qk2  S2",
-    "M0 M1 A0 A1 V M2 M3 Cq2.0 A2 F3 M4 M5 Cq2.1 A4 F5 M6 M7 A6 F7 Tq2.2 Tq2.3 S3- S1 Qq2.0 Qq2.1 W3.0 W3.1 S2",
-    "M0 M1 A0 A1 V M2 M3 Cq2.2 A2 F3 M4 M5 Cq2.3 A4 F5 M6 M7 A6 F7 Tk3a S3- S1 Qq2.2 Qq2.3 W3.2 W3.3 S2",
-    "M0 M1 A0 A1 V M2 M3 Ck3a A2 F3 M4 M5  A4 F5 M6 M7 A6 F7 Tk3b S3- S1   S2",
-    "M0 M1 A0 A1 V M2 M3 Ck3b A2 F3 M4 M5  A4 F5 M6 M7 A6 F7 Tq3.0 S3- S1 Qk3  S2",
-    "M0 M1 A0 A1 V M2 M3 Cq3.0 A2 F3 M4 M5  A4 F5 M6 M7 A6 F7 Tq3.1 S3- S1 Qq3.0  S2",
-    "M0 M1 A0 A1 V M2 M3 Cq3.1 A2 F3 M4 M5  A4 F5 M6 M7 A6 F7 Tq3.2 S3- S1 Qq3.1  S2",
-    "M0 M1 A0 A1 V M2 M3 Cq3.2 A2 F3 M4 M5  A4 F5 M6 M7 A6 F7 Tq3.3 S3- S1 Qq3.2  S2",
-    "M0 M1 A0 A1 V M2 M3 Cq3.3 A2 F3 M4 M5  A4 F5 M6 M7 A6 F7  S3- S1 Qq3.3  S2",
-    "M0 M1 A0 A1 V M2 M3  A2 F3 M4 M5  A4 F5 M6 M7 A6 F7  S3- S1   S2",
-    "M0 M1 A0 A1 V M2 M3  A2 F3 M4 M5  A4 F5 M6 M7 A6 F7  S3- S1   S2",
-    "M0 M1 A0 A1 V M2 M3  A2 F3 M4 M5  A4 F5 M6 M7 A6 F7  S3- S1   S2",
-    "M0 M1 A0 A1 V M2 M3  A2 F3 M4 M5  A4 F5 M6 M7 A6 F7  S3- S1   S2",
-    "M0 M1 A0 A1 V M2 M3  A2 F3 M4 M5  A4 F5 M6 M7 A6 F7  S3- S1   S2 S3"]
+W_MIN = 1e-20
+WARM_UP_MATMULS = 7
+
+UNITS = [
+    (0, 0), (0, 1), (1, 0), (1, 1),
+    (0, 2), (1, 2), (2, 0), (2, 1),
+    (2, 2), (0, 3), (1, 3), (2, 3),
+    (3, 0), (3, 1), (3, 2), (3, 3),
+]
+
+PIECES = {
+    0: ([("q", 1, 0)], []),
+    1: ([("q", 1, 1), ("q", 1, 2)], [("q", 1, 3)]),
+    2: ([("k", 2, 0), ("k", 2, 1)], []),
+    3: ([("q", 2, 0)], []),
+    4: ([("q", 2, 1)], []),
+    5: ([("q", 2, 2)], [("q", 2, 3)]),
+    6: ([("k", 3, 0), ("k", 3, 1)], []),
+    7: ([("q", 3, 0)], []),
+    8: ([("q", 3, 1)], []),
+    9: ([("q", 3, 2)], []),
+    10: ([("q", 3, 3)], []),
+}
+WIDENINGS = {0: [(2, 2), (2, 3), (3, 0), (3, 1)], 1: [(3, 2), (3, 3)]}
 
 
 def tile_sparse_indexer_scores_d3_kernel(tc, q, k_bytes, k_scale, w, out):
@@ -48,211 +52,239 @@ def tile_sparse_indexer_scores_d3_kernel(tc, q, k_bytes, k_scale, w, out):
         keep = ctx.enter_context(tc.tile_pool(name="keep", bufs=1))
         work = ctx.enter_context(tc.tile_pool(name="work", bufs=3))
         ps_t = ctx.enter_context(tc.psum_pool(name="ps_t", bufs=2))
-        ps_a = ctx.enter_context(tc.psum_pool(name="ps_a", bufs=3))
-        ps_d = ctx.enter_context(tc.psum_pool(name="ps_d", bufs=3))
-
+        ps_s = ctx.enter_context(tc.psum_pool(name="ps_s", bufs=3))
+        ps_v = ctx.enter_context(tc.psum_pool(name="ps_v", bufs=3))
         ctx.enter_context(tc.manual_schedule())
 
-        q_v = q.rearrange("(p i) h d -> i p h d", i=NT)
-        kb_v = k_bytes.rearrange("(c p j) d -> c p (j d)", p=P, j=4)
-        ks_v = k_scale.rearrange("(c p j) o -> p c (j o)", p=P, j=4)
-        w_v = w.rearrange("(p i) h -> p (i h)", i=NT)
-        out_v = out.rearrange("(p i) s -> i p s", i=NT)
+        q_rows = q.rearrange("(p i) h d -> i p h d", i=TILES)
+        k_rows = k_bytes.rearrange("(c p j) d -> c p (j d)", p=P, j=4)
+        scale_rows = k_scale.rearrange("(c p j) o -> p c (j o)", p=P, j=4)
+        w_rows = w.rearrange("(p i) h -> p (i h)", i=TILES)
+        out_rows = out.rearrange("(p i) s -> i p s", i=TILES)
 
-        ks = keep.tile([P, NC, 4], F32, name="ks")
-        wb = keep.tile([P, NT * H], BF16, name="wb")
-        kb = [keep.tile([P, 4, D], U8, name=f"kb{c}") for c in range(NC)]
-        qr0 = [keep.tile([P, 2, D], BF16, name=f"qr0_{p}") for p in range(4)]
-        qr = [None] + [keep.tile([P, H, D], BF16, name=f"qr{i}") for i in range(1, NT)]
+        k_raw = [keep.tile([P, 4, D], U8, name=f"kb{c}") for c in range(CHUNKS)]
+        k_sc = keep.tile([P, CHUNKS, 4], F32, name="k_sc")
+        k_wide = [keep.tile([P, 4, D], BF16, name=f"k_wide{c}", align_bytes=64) for c in range(CHUNKS)]
+        k_group = [keep.tile([P, SC, 4], BF16, name=f"kg{c}", align_bytes=64) for c in range(CHUNKS)]
+        k_codes = keep.tile([P, S], U32, name="k_codes", align_bytes=64)
+        k_planes = keep.tile([P, S], U8, name="k_planes", align_bytes=64)
+        q_raw0 = [keep.tile([P, 2, D], BF16, name=f"q_raw0_{p}") for p in range(4)]
+        q_raw = [keep.tile([P, H, D], BF16, name=f"q_raw{i}") for i in range(1, TILES)]
+        q_group = [keep.tile([P, H * P, 4], BF16, name=f"q_group{i}", align_bytes=64) for i in range(TILES)]
+        q_codes = [keep.tile([P, H * P], U32, name=f"q_codes{i}", align_bytes=64) for i in range(TILES)]
+        q_planes = [keep.tile([P, H * P], U8, name=f"q_planes{i}", align_bytes=64) for i in range(TILES)]
+        w_raw = keep.tile([P, TILES * H], BF16, name="w_raw")
+        w_f = keep.tile([P, TILES, H], F32, name="w_f")
+        w_c = keep.tile([P, TILES, H], F32, name="w_c")
+        w_inv = keep.tile([P, TILES, H], F32, name="w_inv")
+        r_relu = keep.tile([P, TILES, 3], F32, name="r_relu")
+        r_sum = keep.tile([P, TILES, 1], F32, name="r_sum")
+        ident = keep.tile([P, P], F32, name="ident")
+        zeros = keep.tile([P, P + SC], BF16, name="zeros")
+        relu0 = keep.tile([P, 1], F32, name="relu0")
 
         def load_k(c):
-            nc.sync.dma_start(out=kb[c][:].rearrange("p j d -> p (j d)"), in_=kb_v[c])
+            nc.sync.dma_start(out=k_raw[c][:].rearrange("p j d -> p (j d)"), in_=k_rows[c])
 
-        def load_q0(p):
-            nc.sync.dma_start(out=qr0[p][:], in_=q_v[0][:, 2 * p : 2 * p + 2, :])
+        def load_q0(pair):
+            nc.sync.dma_start(out=q_raw0[pair][:], in_=q_rows[0][:, 2 * pair : 2 * pair + 2, :])
 
-        for tok in LOADS.split():
-            if tok == "ks":
-                nc.sync.dma_start(out=ks[:], in_=ks_v)
-            elif tok == "wb":
-                nc.sync.dma_start(out=wb[:], in_=w_v)
-            elif tok[0] == "k":
-                load_k(int(tok[1:]))
-            elif tok[:3] == "q0.":
-                load_q0(int(tok[3:]))
+        def load_q(i):
+            nc.sync.dma_start(out=q_raw[i - 1][:], in_=q_rows[i])
+
+        load_k(0)
+        nc.sync.dma_start(out=k_sc[:], in_=scale_rows)
+        load_q0(0)
+        load_q0(1)
+        load_k(1)
+        nc.sync.dma_start(out=w_raw[:], in_=w_rows)
+        load_q0(2)
+        load_q0(3)
+        load_k(2)
+        load_q(1)
+        load_k(3)
+        load_q(2)
+        load_q(3)
+
+        def widen(c, j, on_scalar=False):
+            src = k_raw[c][:, j, :].bitcast(FP8)
+            scale = k_sc[:, c, j : j + 1]
+            if on_scalar:
+                nc.scalar.activation(out=k_wide[c][:, j, :], in_=src, func=ACT.Copy, scale=scale)
             else:
-                nc.sync.dma_start(out=qr[int(tok[1:])][:], in_=q_v[int(tok[1:])])
+                nc.vector.tensor_scalar(out=k_wide[c][:, j, :], in0=src, scalar1=scale, scalar2=None, op0=ALU.mult)
 
-        ident = keep.tile([P, P], F32, name="ident")
-        make_identity(nc, ident[:])
-        warm = keep.tile([P, 1], F32, name="warm")
-        nc.vector.memset(warm[:], 0.0)
-        warm2 = keep.tile([P, 1], F32, name="warm2")
-        nc.scalar.activation(out=warm2[:], in_=warm[:], func=ACT.Relu)
+        turned = {}
 
-        kg = [keep.tile([P, SC, 4], BF16, name=f"kg{c}", align_bytes=64) for c in range(NC)]
-        kw = [keep.tile([P, 4, D], BF16, name=f"kw{c}", align_bytes=64) for c in range(NC)]
-        kc = keep.tile([P, S], U32, name="kc", align_bytes=64)
-        ksc = keep.tile([P, S], U8, name="ksc", align_bytes=64)
-        qg = [keep.tile([P, H * P, 4], BF16, name=f"qg{i}", align_bytes=64) for i in range(NT)]
-        qc = [keep.tile([P, H * P], U32, name=f"qc{i}", align_bytes=64) for i in range(NT)]
-        qsc = [keep.tile([P, H * P], U8, name=f"qsc{i}", align_bytes=64) for i in range(NT)]
-
-        def k_widen(c, j, on_act):
-            src = kb[c][:, j, :].bitcast(FP8)
-            sc = ks[:, c, j : j + 1]
-            if on_act:
-                nc.scalar.activation(out=kw[c][:, j, :], in_=src, func=ACT.Copy, scale=sc)
-            else:
-                nc.vector.tensor_scalar(out=kw[c][:, j, :], in0=src, scalar1=sc, scalar2=None, op0=ALU.mult)
-
-        def k_turn(c, pair, pool=ps_t, tag="xt"):
-            xt = pool.tile([P, 4, P], F32, name=tag, tag=tag)
-            for jj in range(2):
-                words = kw[c][:, 2 * pair + jj, :].bitcast(F32)
-                for u in range(2):
-                    nc.tensor.transpose(xt[:, 2 * jj + u, :], words[:, u::2], ident[:])
-            return xt
-
-        def k_out(c, pair, xt, on_act):
-            dst = kg[c][:].rearrange("p n e -> p (n e)").bitcast(F32).rearrange("p (r x) -> p r x", x=8)
-            dst = dst[:, :, 4 * pair : 4 * pair + 4]
-            src = xt[:].rearrange("p x r -> p r x")
-            if on_act:
-                nc.scalar.copy(out=dst, in_=src)
-            else:
-                nc.vector.tensor_copy(out=dst, in_=src)
-
-        def k_quant(c):
-            cols = slice(c * SC, (c + 1) * SC)
-            nc.vector.quantize_mx(
-                out=kc[:, cols].bitcast(FP8X4), scales=ksc[:, cols], in_=kg[c][:].rearrange("p n e -> p (n e)")
-            )
-
-        def q_turn(i, p, pool=ps_t, tag="xt"):
-            xt = pool.tile([P, 4, P], F32, name=tag, tag=tag)
-            for hh in range(2):
-                raw = qr0[p][:, hh, :] if i == 0 else qr[i][:, 2 * p + hh, :]
-                words = raw.bitcast(F32)
-                for u in range(2):
-                    nc.tensor.transpose(xt[:, 2 * hh + u, :], words[:, u::2], ident[:])
-            return xt
-
-        def q_out(i, p, xt, on_act):
-            dst = qg[i][:, 256 * p : 256 * p + 256, :].rearrange("p n e -> p (n e)").bitcast(F32)
-            dst = dst.rearrange("p (h r u) -> p h r u", h=2, u=2)
-            src = xt[:].rearrange("p (h u) r -> p h r u", u=2)
-            if on_act:
-                nc.scalar.copy(out=dst, in_=src)
-            else:
-                nc.vector.tensor_copy(out=dst, in_=src)
-
-        def q_quant(i, p):
-            cols = slice(256 * p, 256 * p + 256)
-            nc.vector.quantize_mx(
-                out=qc[i][:, cols].bitcast(FP8X4),
-                scales=qsc[i][:, cols],
-                in_=qg[i][:, cols, :].rearrange("p n e -> p (n e)"),
-            )
-
-        wf = keep.tile([P, NT, H], F32, name="wf")
-        wc = keep.tile([P, NT, H], F32, name="wc")
-        rc = keep.tile([P, NT, H], F32, name="rc")
-        ra = keep.tile([P, NT, 3], F32, name="ra")
-        rz = keep.tile([P, NT, 1], F32, name="rz")
-
-        def mx(i, c, h, pool, tag):
-            ps = pool.tile([P, SC], F32, name=tag, tag=tag)
-            qs = slice(h * P, (h + 1) * P)
-            cs = slice(c * SC, (c + 1) * SC)
-            nc.tensor.matmul_mx(
-                out=ps[:],
-                lhsT=qc[i][:, qs].bitcast(FP8X4),
-                lhsT_scale=qsc[i][:, qs],
-                rhs=kc[:, cs].bitcast(FP8X4),
-                rhs_scale=ksc[:, cs],
-                start=True,
-                stop=True,
-            )
-            return ps
-
-        def relu_scaled(ps, col, tag):
-            a = work.tile([P, SC], F32, name=tag, tag=tag)
-            nc.scalar.activation(out=a[:], in_=ps[:], func=ACT.Relu, scale=col)
-            return a
-
-        def relu_add(ps, a, tag):
-            z = work.tile([P, SC], F32, name=tag, tag=tag)
-            nc.vector.scalar_tensor_tensor(out=z[:], in0=ps[:], scalar=0.0, in1=a[:], op0=ALU.max, op1=ALU.add)
-            return z
-
-        def mul_add(z, col, y, tag):
-            o = work.tile([P, SC], F32, name=tag, tag=tag)
-            nc.vector.scalar_tensor_tensor(out=o[:], in0=z[:], scalar=col, in1=y[:], op0=ALU.mult, op1=ALU.add)
-            return o
-
-        units = UNITS
-        PS = {"x": (ps_t, "xt"), "a": (ps_a, "pa"), "d": (ps_d, "pd")}
-        R_ = {}
-
-        def kq(tok):
-            if tok[0] == "k":
-                return k_turn, k_out, int(tok[1]), "ab".index(tok[2])
-            return q_turn, q_out, int(tok[1]), int(tok[3])
-
-        for n, text in enumerate(PROGRAM):
-            u = n - 1
-            for tok in text.split():
-                op, arg = tok[0], tok[1:]
-                if op in "Ww":
-                    k_widen(int(arg[0]), int(arg[2]), op == "w")
-                elif op == "T":
-                    bank = "x"
-                    if arg[-1] in "xad" and arg[-2] == "/":
-                        bank = arg[-1]
-                        arg = arg[:-2]
-                    f, g, a, b = kq(arg)
-                    R_[arg] = f(a, b, PS[bank][0], PS[bank][1])
-                elif op in "CD":
-                    f, g, a, b = kq(arg)
-                    g(a, b, R_[arg], op == "C")
-                elif op == "Q":
-                    if arg[0] == "k":
-                        k_quant(int(arg[1]))
-                    else:
-                        q_quant(int(arg[1]), int(arg[3]))
-                elif op == "P":
-                    if arg == "0":
-                        nc.vector.tensor_copy(out=wf[:].rearrange("p i h -> p (i h)"), in_=wb[:])
-                    elif arg == "1":
-                        nc.vector.tensor_scalar(out=wc[:], in0=wf[:], scalar1=TINY, scalar2=None, op0=ALU.max)
-                    elif arg == "2":
-                        nc.vector.reciprocal(out=rc[:], in_=wc[:])
-                    elif arg == "3":
-                        nc.vector.tensor_tensor(out=ra[:], in0=wf[:, :, 2:8:2], in1=rc[:, :, 3:8:2], op=ALU.mult)
-                    else:
-                        nc.vector.tensor_tensor(out=rz[:], in0=wc[:, :, 3:4], in1=rc[:, :, 5:6], op=ALU.mult)
+        def turn(piece, pool=ps_t, tag="bank_t"):
+            kind, n, half = piece
+            bank = pool.tile([P, 4, P], F32, name=tag, tag=tag)
+            for x in range(2):
+                if kind == "k":
+                    rows = k_wide[n][:, 2 * half + x, :]
+                elif n == 0:
+                    rows = q_raw0[half][:, x, :]
                 else:
-                    hs = arg.replace("-", "")
-                    v = u - (len(arg) - len(hs))
-                    h = int(hs) if hs else 0
-                    i, c = units[v]
-                    if op == "M":
-                        bank = "d" if h in (3, 5, 7) else "a"
-                        R_[("m", v, h)] = mx(i, c, h, PS[bank][0], PS[bank][1])
-                    elif op == "A":
-                        col = ra[:, i, h // 2 - 1 : h // 2] if h > 1 else wf[:, i, h : h + 1]
-                        R_[("a", v, h)] = relu_scaled(R_[("m", v, h)], col, "a%d" % h)
-                    elif op == "F":
-                        R_[("z", v, h)] = relu_add(R_[("m", v, h)], R_[("a", v, h - 1)], "z%d" % h)
-                    elif op == "V":
-                        vt = keep.tile([P, SC], F32, name="v", tag="v")
-                        nc.gpsimd.tensor_tensor(out=vt[:], in0=R_[("a", v, 0)][:], in1=R_[("a", v, 1)][:], op=ALU.add)
-                        R_[("v", v)] = vt
-                    elif op == "S" and h == 1:
-                        R_[("s1", v)] = mul_add(R_[("z", v, 3)], rz[:, i, 0:1], R_[("z", v, 5)], "s1")
-                    elif op == "S" and h == 2:
-                        R_[("s2", v)] = mul_add(R_[("z", v, 7)], wc[:, i, 7:8], R_[("v", v)], "s2")
-                    elif op == "S" and h == 3:
-                        o = mul_add(R_[("s1", v)], wc[:, i, 5:6], R_[("s2", v)], "o")
-                        nc.sync.dma_start(out=out_v[i][:, c * SC : (c + 1) * SC], in_=o[:])
+                    rows = q_raw[n - 1][:, 2 * half + x, :]
+                words = rows.bitcast(F32)
+                for u in range(2):
+                    nc.tensor.transpose(bank[:, 2 * x + u, :], words[:, u::2], ident[:])
+            turned[piece] = bank
+
+        def copy_out(piece, on_vector=False):
+            kind, n, half = piece
+            if kind == "k":
+                words = k_group[n][:].rearrange("p n e -> p (n e)").bitcast(F32)
+                dst = words.rearrange("p (r x) -> p r x", x=8)[:, :, 4 * half : 4 * half + 4]
+                src = turned[piece][:].rearrange("p x r -> p r x")
+            else:
+                words = q_group[n][:, 2 * P * half : 2 * P * (half + 1), :].rearrange("p n e -> p (n e)").bitcast(F32)
+                dst = words.rearrange("p (h r u) -> p h r u", h=2, u=2)
+                src = turned[piece][:].rearrange("p (h u) r -> p h r u", u=2)
+            if on_vector:
+                nc.vector.tensor_copy(out=dst, in_=src)
+            else:
+                nc.scalar.copy(out=dst, in_=src)
+
+        def quantize(piece):
+            kind, n, half = piece
+            if kind == "q":
+                cols = slice(2 * P * half, 2 * P * (half + 1))
+                codes, planes, src = q_codes[n][:, cols], q_planes[n][:, cols], q_group[n][:, cols, :]
+            elif half == 1:
+                cols = slice(SC * n, SC * (n + 1))
+                codes, planes, src = k_codes[:, cols], k_planes[:, cols], k_group[n][:]
+            else:
+                return
+            nc.vector.quantize_mx(out=codes.bitcast(FP8X4), scales=planes, in_=src.rearrange("p n e -> p (n e)"))
+
+        nc.vector.memset(zeros[:], 0.0)
+        nc.scalar.activation(out=relu0[:], in_=zeros[:, 0:1], func=ACT.Relu)
+        make_identity(nc, ident[:])
+        idle = ps_v.tile([P, SC], F32, name="bank_v", tag="bank_v")
+        for m in range(WARM_UP_MATMULS):
+            nc.tensor.matmul(idle[:], lhsT=zeros[:, 0:P], rhs=zeros[:, P:], start=True, stop=True)
+
+        q0 = [("q", 0, pair) for pair in range(4)]
+        k0 = [("k", 0, half) for half in range(2)]
+        k1 = [("k", 1, half) for half in range(2)]
+        widen(0, 0)
+        widen(0, 1)
+        widen(0, 2, on_scalar=True)
+        widen(0, 3)
+        turn(q0[0], ps_s, "bank_s")
+        turn(k0[0])
+        turn(q0[1], ps_s, "bank_s")
+        turn(k0[1])
+        turn(q0[2], ps_v, "bank_v")
+        copy_out(q0[0], on_vector=True)
+        widen(1, 0)
+        widen(1, 1, on_scalar=True)
+        quantize(q0[0])
+        nc.vector.tensor_copy(out=w_f[:].rearrange("p i h -> p (i h)"), in_=w_raw[:])
+        widen(1, 2)
+        nc.vector.tensor_scalar(out=w_c[:], in0=w_f[:], scalar1=W_MIN, scalar2=None, op0=ALU.max)
+        widen(1, 3)
+        nc.vector.reciprocal(out=w_inv[:], in_=w_c[:])
+        copy_out(k0[0])
+        widen(2, 0)
+        widen(2, 1, on_scalar=True)
+        copy_out(k0[1], on_vector=True)
+        copy_out(q0[1])
+        turn(k1[0])
+        turn(q0[3], ps_s, "bank_s")
+        turn(k1[1])
+        quantize(k0[1])
+        nc.vector.tensor_tensor(out=r_relu[:], in0=w_f[:, :, 2:8:2], in1=w_inv[:, :, 3:8:2], op=ALU.mult)
+        copy_out(q0[3], on_vector=True)
+        quantize(q0[1])
+        nc.vector.tensor_tensor(out=r_sum[:], in0=w_c[:, :, 3:4], in1=w_inv[:, :, 5:6], op=ALU.mult)
+        quantize(q0[3])
+        copy_out(k1[1], on_vector=True)
+        copy_out(k1[0])
+        copy_out(q0[2])
+        quantize(q0[2])
+        quantize(k1[1])
+
+        state = {}
+
+        def store_sum(n):
+            i, c = UNITS[n]
+            s1, s2 = state[n]
+            result = work.tile([P, SC], F32, name="result", tag="result")
+            nc.vector.scalar_tensor_tensor(
+                out=result[:], in0=s1[:], scalar=w_c[:, i, 5:6], in1=s2[:], op0=ALU.mult, op1=ALU.add
+            )
+            nc.sync.dma_start(out=out_rows[i][:, c * SC : (c + 1) * SC], in_=result[:])
+
+        def unit(n):
+            i, c = UNITS[n]
+            early, late = PIECES.get(n, ([], []))
+            keys = slice(c * SC, (c + 1) * SC)
+
+            banks = []
+            for h in range(H):
+                if h in (3, 5, 7):
+                    bank = ps_v.tile([P, SC], F32, name="bank_v", tag="bank_v")
+                else:
+                    bank = ps_s.tile([P, SC], F32, name="bank_s", tag="bank_s")
+                rows = slice(h * P, (h + 1) * P)
+                nc.tensor.matmul_mx(
+                    out=bank[:],
+                    lhsT=q_codes[i][:, rows].bitcast(FP8X4),
+                    lhsT_scale=q_planes[i][:, rows],
+                    rhs=k_codes[:, keys].bitcast(FP8X4),
+                    rhs_scale=k_planes[:, keys],
+                    start=True,
+                    stop=True,
+                )
+                banks.append(bank)
+                if h == 0:
+                    for piece in early:
+                        turn(piece)
+            for piece in late:
+                turn(piece)
+
+            a = {}
+            for h in (0, 1, 2, 4, 6):
+                factor = w_f[:, i, h : h + 1] if h < 2 else r_relu[:, i, h // 2 - 1 : h // 2]
+                a_h = work.tile([P, SC], F32, name=f"a{h}", tag=f"a{h}")
+                nc.scalar.activation(out=a_h[:], in_=banks[h][:], func=ACT.Relu, scale=factor)
+                a[h] = a_h
+                if h == 0:
+                    for piece in early:
+                        copy_out(piece)
+            for piece in late:
+                copy_out(piece)
+
+            v = keep.tile([P, SC], F32, name="v", tag="v")
+            nc.gpsimd.tensor_tensor(out=v[:], in0=a[0][:], in1=a[1][:], op=ALU.add)
+
+            z = {}
+            for h in (3, 5, 7):
+                z_h = work.tile([P, SC], F32, name=f"z{h}", tag=f"z{h}")
+                nc.vector.scalar_tensor_tensor(
+                    out=z_h[:], in0=banks[h][:], scalar=0.0, in1=a[h - 1][:], op0=ALU.max, op1=ALU.add
+                )
+                z[h] = z_h
+            for piece in early:
+                quantize(piece)
+            if n > 0:
+                store_sum(n - 1)
+            s1 = work.tile([P, SC], F32, name="s1", tag="s1")
+            nc.vector.scalar_tensor_tensor(
+                out=s1[:], in0=z[3][:], scalar=r_sum[:, i, :], in1=z[5][:], op0=ALU.mult, op1=ALU.add
+            )
+            for piece in late:
+                quantize(piece)
+            for cj in WIDENINGS.get(n, []):
+                widen(cj[0], cj[1])
+            s2 = work.tile([P, SC], F32, name="s2", tag="s2")
+            nc.vector.scalar_tensor_tensor(
+                out=s2[:], in0=z[7][:], scalar=w_c[:, i, 7:8], in1=v[:], op0=ALU.mult, op1=ALU.add
+            )
+            state[n] = (s1, s2)
+
+        for n in range(len(UNITS)):
+            unit(n)
+        store_sum(len(UNITS) - 1)

@@ -63,7 +63,8 @@ def tile_sparse_indexer_scores_d3_kernel(tc, q, k_bytes, k_scale, w, out):
         out_rows = out.rearrange("(p i) s -> i p s", i=TILES)
 
         k_raw = [keep.tile([P, 4, D], U8, name=f"kb{c}") for c in range(CHUNKS)]
-        k_sc = keep.tile([P, CHUNKS, 4], F32, name="k_sc")
+        k_sc0 = keep.tile([P, 4], F32, name="k_sc0")
+        k_sc = keep.tile([P, CHUNKS - 1, 4], F32, name="k_sc")
         k_wide = [keep.tile([P, 4, D], BF16, name=f"k_wide{c}", align_bytes=64) for c in range(CHUNKS)]
         k_group = [keep.tile([P, SC, 4], BF16, name=f"kg{c}", align_bytes=64) for c in range(CHUNKS)]
         k_codes = keep.tile([P, S], U32, name="k_codes", align_bytes=64)
@@ -93,10 +94,11 @@ def tile_sparse_indexer_scores_d3_kernel(tc, q, k_bytes, k_scale, w, out):
             nc.sync.dma_start(out=q_raw[i - 1][:], in_=q_rows[i])
 
         load_k(0)
-        nc.sync.dma_start(out=k_sc[:], in_=scale_rows)
+        nc.sync.dma_start(out=k_sc0[:], in_=scale_rows[:, 0, :])
         load_q0(0)
         load_q0(1)
         load_k(1)
+        nc.sync.dma_start(out=k_sc[:], in_=scale_rows[:, 1:CHUNKS, :])
         nc.sync.dma_start(out=w_raw[:], in_=w_rows)
         load_q0(2)
         load_q0(3)
@@ -108,7 +110,7 @@ def tile_sparse_indexer_scores_d3_kernel(tc, q, k_bytes, k_scale, w, out):
 
         def widen(c, j, on_scalar=False):
             src = k_raw[c][:, j, :].bitcast(FP8)
-            scale = k_sc[:, c, j : j + 1]
+            scale = k_sc0[:, j : j + 1] if c == 0 else k_sc[:, c - 1, j : j + 1]
             if on_scalar:
                 nc.scalar.activation(out=k_wide[c][:, j, :], in_=src, func=ACT.Copy, scale=scale)
             else:
@@ -208,14 +210,18 @@ def tile_sparse_indexer_scores_d3_kernel(tc, q, k_bytes, k_scale, w, out):
 
         state = {}
 
-        def store_sum(n):
+        def store_sum(n, parts=1):
             i, c = UNITS[n]
             s1, s2 = state[n]
-            result = work.tile([P, SC], F32, name="result", tag="result")
-            nc.vector.scalar_tensor_tensor(
-                out=result[:], in0=s1[:], scalar=w_c[:, i, 5:6], in1=s2[:], op0=ALU.mult, op1=ALU.add
-            )
-            nc.sync.dma_start(out=out_rows[i][:, c * SC : (c + 1) * SC], in_=result[:])
+            width = SC // parts
+            for part in range(parts):
+                cols = slice(part * width, (part + 1) * width)
+                result = work.tile([P, width], F32, name="result", tag="result")
+                nc.vector.scalar_tensor_tensor(
+                    out=result[:], in0=s1[:, cols], scalar=w_c[:, i, 5:6], in1=s2[:, cols], op0=ALU.mult, op1=ALU.add
+                )
+                keys = slice(c * SC + part * width, c * SC + (part + 1) * width)
+                nc.sync.dma_start(out=out_rows[i][:, keys], in_=result[:])
 
         def unit(n):
             i, c = UNITS[n]
@@ -257,28 +263,29 @@ def tile_sparse_indexer_scores_d3_kernel(tc, q, k_bytes, k_scale, w, out):
             for piece in late:
                 copy_out(piece)
 
-            v = keep.tile([P, SC], F32, name="v", tag="v")
+            z5 = keep.tile([P, SC], F32, name=f"x{n % 2}", tag=f"x{n % 2}")
+            v = keep.tile([P, SC], F32, name=f"x{(n + 1) % 2}", tag=f"x{(n + 1) % 2}")
             nc.gpsimd.tensor_tensor(out=v[:], in0=a[0][:], in1=a[1][:], op=ALU.add)
 
             z = {}
             for h in (3, 5, 7):
-                z_h = work.tile([P, SC], F32, name=f"z{h}", tag=f"z{h}")
+                z_h = z5 if h == 5 else work.tile([P, SC], F32, name=f"z{h}", tag=f"z{h}")
                 nc.vector.scalar_tensor_tensor(
                     out=z_h[:], in0=banks[h][:], scalar=0.0, in1=a[h - 1][:], op0=ALU.max, op1=ALU.add
                 )
                 z[h] = z_h
             for piece in early:
                 quantize(piece)
-            if n > 0:
+            if 0 < n < len(UNITS) - 1:
                 store_sum(n - 1)
-            s1 = work.tile([P, SC], F32, name="s1", tag="s1")
-            nc.vector.scalar_tensor_tensor(
-                out=s1[:], in0=z[3][:], scalar=r_sum[:, i, :], in1=z[5][:], op0=ALU.mult, op1=ALU.add
-            )
             for piece in late:
                 quantize(piece)
             for cj in WIDENINGS.get(n, []):
                 widen(cj[0], cj[1])
+            s1 = work.tile([P, SC], F32, name="s1", tag="s1")
+            nc.vector.scalar_tensor_tensor(
+                out=s1[:], in0=z[3][:], scalar=r_sum[:, i, :], in1=z[5][:], op0=ALU.mult, op1=ALU.add
+            )
             s2 = work.tile([P, SC], F32, name="s2", tag="s2")
             nc.vector.scalar_tensor_tensor(
                 out=s2[:], in0=z[7][:], scalar=w_c[:, i, 7:8], in1=v[:], op0=ALU.mult, op1=ALU.add
@@ -287,4 +294,5 @@ def tile_sparse_indexer_scores_d3_kernel(tc, q, k_bytes, k_scale, w, out):
 
         for n in range(len(UNITS)):
             unit(n)
-        store_sum(len(UNITS) - 1)
+        store_sum(len(UNITS) - 2)
+        store_sum(len(UNITS) - 1, parts=2)

@@ -21,7 +21,6 @@ CHUNKS = S // SC
 FLOPS = 2 * T * H * D * S + 3 * T * H * S
 
 W_MIN = 1e-20
-WARM_UP_MATMULS = 7
 
 UNITS = [
     (0, 0), (0, 1), (1, 0), (1, 1),
@@ -81,7 +80,7 @@ def tile_sparse_indexer_scores_d3_kernel(tc, q, k_bytes, k_scale, w, out):
         r_relu = keep.tile([P, TILES, 3], F32, name="r_relu")
         r_sum = keep.tile([P, TILES, 1], F32, name="r_sum")
         ident = keep.tile([P, P], F32, name="ident")
-        zeros = keep.tile([P, P + SC], BF16, name="zeros")
+        zeros = keep.tile([P, 1], BF16, name="zeros")
         relu0 = keep.tile([P, 1], F32, name="relu0")
 
         def load_k(c):
@@ -161,11 +160,8 @@ def tile_sparse_indexer_scores_d3_kernel(tc, q, k_bytes, k_scale, w, out):
             nc.vector.quantize_mx(out=codes.bitcast(FP8X4), scales=planes, in_=src.rearrange("p n e -> p (n e)"))
 
         nc.vector.memset(zeros[:], 0.0)
-        nc.scalar.activation(out=relu0[:], in_=zeros[:, 0:1], func=ACT.Relu)
+        nc.scalar.activation(out=relu0[:], in_=zeros[:], func=ACT.Relu)
         make_identity(nc, ident[:])
-        idle = ps_v.tile([P, SC], F32, name="bank_v", tag="bank_v")
-        for m in range(WARM_UP_MATMULS):
-            nc.tensor.matmul(idle[:], lhsT=zeros[:, 0:P], rhs=zeros[:, P:], start=True, stop=True)
 
         q0 = [("q", 0, pair) for pair in range(4)]
         k0 = [("k", 0, half) for half in range(2)]

from contextlib import ExitStack

import concourse.mybir as mybir
from concourse.masks import make_identity

F32 = mybir.dt.float32
BF16 = mybir.dt.bfloat16
U32 = mybir.dt.uint32
U8 = mybir.dt.uint8
FP8 = mybir.dt.float8_e4m3fn
FP8X4 = mybir.dt.float8_e4m3fn_x4
ACT = mybir.ActivationFunctionType
ALU = mybir.AluOpType

P = 128
T, H, D, S = 512, 8, 512, 2048
TILES = T // P
SC = 512
CHUNKS = S // SC

FLOPS = 2 * T * H * D * S + 3 * T * H * S

W_MIN = 1e-20

UNITS = [
    (0, 0), (0, 1), (1, 0), (1, 1),
    (0, 2), (1, 2), (2, 0), (2, 1),
    (2, 2), (0, 3), (1, 3), (2, 3),
    (3, 0), (3, 1), (3, 2), (3, 3),
]

PIECES = {
    0: ([("q", 1, 0)], []),
    1: ([("q", 1, 1), ("q", 1, 2)], [("q", 1, 3)]),
    2: ([("k", 2, 0), ("k", 2, 1)], []),
    3: ([("q", 2, 0)], []),
    4: ([("q", 2, 1)], []),
    5: ([("q", 2, 2)], [("q", 2, 3)]),
    6: ([("k", 3, 0), ("k", 3, 1)], []),
    7: ([("q", 3, 0)], []),
    8: ([("q", 3, 1)], []),
    9: ([("q", 3, 2)], []),
    10: ([("q", 3, 3)], []),
}
WIDENINGS = {0: [(2, 2), (2, 3), (3, 0), (3, 1)], 1: [(3, 2), (3, 3)]}


def tile_sparse_indexer_scores_d3_kernel(tc, q, k_bytes, k_scale, w, out):
    nc = tc.nc
    with ExitStack() as ctx:
        keep = ctx.enter_context(tc.tile_pool(name="keep", bufs=1))
        work = ctx.enter_context(tc.tile_pool(name="work", bufs=3))
        ps_t = ctx.enter_context(tc.psum_pool(name="ps_t", bufs=2))
        ps_s = ctx.enter_context(tc.psum_pool(name="ps_s", bufs=3))
        ps_v = ctx.enter_context(tc.psum_pool(name="ps_v", bufs=3))
        ctx.enter_context(tc.manual_schedule())

        q_rows = q.rearrange("(p i) h d -> i p h d", i=TILES)
        k_rows = k_bytes.rearrange("(c p j) d -> c p (j d)", p=P, j=4)
        scale_rows = k_scale.rearrange("(c p j) o -> p c (j o)", p=P, j=4)
        w_rows = w.rearrange("(p i) h -> p (i h)", i=TILES)
        out_rows = out.rearrange("(p i) s -> i p s", i=TILES)

        k_raw = [keep.tile([P, 4, D], U8, name=f"kb{c}") for c in range(CHUNKS)]
        k_sc0 = keep.tile([P, 4], F32, name="k_sc0")
        k_sc = keep.tile([P, CHUNKS - 1, 4], F32, name="k_sc")
        k_wide = [keep.tile([P, 4, D], BF16, name=f"k_wide{c}", align_bytes=64) for c in range(CHUNKS)]
        k_group = [keep.tile([P, SC, 4], BF16, name=f"kg{c}", align_bytes=64) for c in range(CHUNKS)]
        k_codes = keep.tile([P, S], U32, name="k_codes", align_bytes=64)
        k_planes = keep.tile([P, S], U8, name="k_planes", align_bytes=64)
        q_raw0 = [keep.tile([P, 2, D], BF16, name=f"q_raw0_{p}") for p in range(4)]
        q_raw = [keep.tile([P, H, D], BF16, name=f"q_raw{i}") for i in range(1, TILES)]
        q_group = [keep.tile([P, H * P, 4], BF16, name=f"q_group{i}", align_bytes=64) for i in range(TILES)]
        q_codes = [keep.tile([P, H * P], U32, name=f"q_codes{i}", align_bytes=64) for i in range(TILES)]
        q_planes = [keep.tile([P, H * P], U8, name=f"q_planes{i}", align_bytes=64) for i in range(TILES)]
        w_raw = keep.tile([P, TILES * H], BF16, name="w_raw")
        w_f = keep.tile([P, TILES, H], F32, name="w_f")
        w_c = keep.tile([P, TILES, H], F32, name="w_c")
        w_inv = keep.tile([P, TILES, H], F32, name="w_inv")
        r_relu = keep.tile([P, TILES, 3], F32, name="r_relu")
        r_sum = keep.tile([P, TILES, 1], F32, name="r_sum")
        ident = keep.tile([P, P], F32, name="ident")
        zeros = keep.tile([P, 1], BF16, name="zeros")
        relu0 = keep.tile([P, 1], F32, name="relu0")

        def load_k(c):
            nc.sync.dma_start(out=k_raw[c][:].rearrange("p j d -> p (j d)"), in_=k_rows[c])

        def load_q0(pair):
            nc.sync.dma_start(out=q_raw0[pair][:], in_=q_rows[0][:, 2 * pair : 2 * pair + 2, :])

        def load_q(i):
            nc.sync.dma_start(out=q_raw[i - 1][:], in_=q_rows[i])

        load_k(0)
        nc.sync.dma_start(out=k_sc0[:], in_=scale_rows[:, 0, :])
        load_q0(0)
        load_q0(1)
        load_k(1)
        nc.sync.dma_start(out=k_sc[:], in_=scale_rows[:, 1:CHUNKS, :])
        nc.sync.dma_start(out=w_raw[:], in_=w_rows)
        load_q0(2)
        load_q0(3)
        load_k(2)
        load_q(1)
        load_k(3)
        load_q(2)
        load_q(3)

        def widen(c, j, on_scalar=False):
            src = k_raw[c][:, j, :].bitcast(FP8)
            scale = k_sc0[:, j : j + 1] if c == 0 else k_sc[:, c - 1, j : j + 1]
            if on_scalar:
                nc.scalar.activation(out=k_wide[c][:, j, :], in_=src, func=ACT.Copy, scale=scale)
            else:
                nc.vector.tensor_scalar(out=k_wide[c][:, j, :], in0=src, scalar1=scale, scalar2=None, op0=ALU.mult)

        turned = {}

        def turn(piece, pool=ps_t, tag="bank_t"):
            kind, n, half = piece
            bank = pool.tile([P, 4, P], F32, name=tag, tag=tag)
            for x in range(2):
                if kind == "k":
                    rows = k_wide[n][:, 2 * half + x, :]
                elif n == 0:
                    rows = q_raw0[half][:, x, :]
                else:
                    rows = q_raw[n - 1][:, 2 * half + x, :]
                words = rows.bitcast(F32)
                for u in range(2):
                    nc.tensor.transpose(bank[:, 2 * x + u, :], words[:, u::2], ident[:])
            turned[piece] = bank

        def copy_out(piece, on_vector=False):
            kind, n, half = piece
            if kind == "k":
                words = k_group[n][:].rearrange("p n e -> p (n e)").bitcast(F32)
                dst = words.rearrange("p (r x) -> p r x", x=8)[:, :, 4 * half : 4 * half + 4]
                src = turned[piece][:].rearrange("p x r -> p r x")
            else:
                words = q_group[n][:, 2 * P * half : 2 * P * (half + 1), :].rearrange("p n e -> p (n e)").bitcast(F32)
                dst = words.rearrange("p (h r u) -> p h r u", h=2, u=2)
                src = turned[piece][:].rearrange("p (h u) r -> p h r u", u=2)
            if on_vector:
                nc.vector.tensor_copy(out=dst, in_=src)
            else:
                nc.scalar.copy(out=dst, in_=src)

        def quantize(piece):
            kind, n, half = piece
            if kind == "q":
                cols = slice(2 * P * half, 2 * P * (half + 1))
                codes, planes, src = q_codes[n][:, cols], q_planes[n][:, cols], q_group[n][:, cols, :]
            elif half == 1:
                cols = slice(SC * n, SC * (n + 1))
                codes, planes, src = k_codes[:, cols], k_planes[:, cols], k_group[n][:]
            else:
                return
            nc.vector.quantize_mx(out=codes.bitcast(FP8X4), scales=planes, in_=src.rearrange("p n e -> p (n e)"))

        nc.vector.memset(zeros[:], 0.0)
        nc.scalar.activation(out=relu0[:], in_=zeros[:], func=ACT.Relu)
        make_identity(nc, ident[:])

        q0 = [("q", 0, pair) for pair in range(4)]
        k0 = [("k", 0, half) for half in range(2)]
        k1 = [("k", 1, half) for half in range(2)]
        widen(0, 0)
        widen(0, 1)
        widen(0, 2, on_scalar=True)
        widen(0, 3)
        turn(q0[0], ps_s, "bank_s")
        turn(k0[0])
        turn(q0[1], ps_s, "bank_s")
        turn(k0[1])
        turn(q0[2], ps_v, "bank_v")
        copy_out(q0[0], on_vector=True)
        widen(1, 0)
        widen(1, 1, on_scalar=True)
        quantize(q0[0])
        nc.vector.tensor_copy(out=w_f[:].rearrange("p i h -> p (i h)"), in_=w_raw[:])
        widen(1, 2)
        nc.vector.tensor_scalar(out=w_c[:], in0=w_f[:], scalar1=W_MIN, scalar2=None, op0=ALU.max)
        widen(1, 3)
        nc.vector.reciprocal(out=w_inv[:], in_=w_c[:])
        copy_out(k0[0])
        widen(2, 0)
        widen(2, 1, on_scalar=True)
        copy_out(k0[1], on_vector=True)
        copy_out(q0[1])
        turn(k1[0])
        turn(q0[3], ps_s, "bank_s")
        turn(k1[1])
        quantize(k0[1])
        nc.vector.tensor_tensor(out=r_relu[:], in0=w_f[:, :, 2:8:2], in1=w_inv[:, :, 3:8:2], op=ALU.mult)
        copy_out(q0[3], on_vector=True)
        quantize(q0[1])
        nc.vector.tensor_tensor(out=r_sum[:], in0=w_c[:, :, 3:4], in1=w_inv[:, :, 5:6], op=ALU.mult)
        quantize(q0[3])
        copy_out(k1[1], on_vector=True)
        copy_out(k1[0])
        copy_out(q0[2])
        quantize(q0[2])
        quantize(k1[1])

        state = {}

        def store_sum(n, parts=1):
            i, c = UNITS[n]
            s1, s2 = state[n]
            width = SC // parts
            for part in range(parts):
                cols = slice(part * width, (part + 1) * width)
                result = work.tile([P, width], F32, name="result", tag="result")
                nc.vector.scalar_tensor_tensor(
                    out=result[:], in0=s1[:, cols], scalar=w_c[:, i, 5:6], in1=s2[:, cols], op0=ALU.mult, op1=ALU.add
                )
                keys = slice(c * SC + part * width, c * SC + (part + 1) * width)
                nc.sync.dma_start(out=out_rows[i][:, keys], in_=result[:])

        def unit(n):
            i, c = UNITS[n]
            early, late = PIECES.get(n, ([], []))
            keys = slice(c * SC, (c + 1) * SC)

            banks = []
            for h in range(H):
                if h in (3, 5, 7):
                    bank = ps_v.tile([P, SC], F32, name="bank_v", tag="bank_v")
                else:
                    bank = ps_s.tile([P, SC], F32, name="bank_s", tag="bank_s")
                rows = slice(h * P, (h + 1) * P)
                nc.tensor.matmul_mx(
                    out=bank[:],
                    lhsT=q_codes[i][:, rows].bitcast(FP8X4),
                    lhsT_scale=q_planes[i][:, rows],
                    rhs=k_codes[:, keys].bitcast(FP8X4),
                    rhs_scale=k_planes[:, keys],
                    start=True,
                    stop=True,
                )
                banks.append(bank)
                if h == 0:
                    for piece in early:
                        turn(piece)
            for piece in late:
                turn(piece)

            a = {}
            for h in (0, 1, 2, 4, 6):
                factor = w_f[:, i, h : h + 1] if h < 2 else r_relu[:, i, h // 2 - 1 : h // 2]
                a_h = work.tile([P, SC], F32, name=f"a{h}", tag=f"a{h}")
                nc.scalar.activation(out=a_h[:], in_=banks[h][:], func=ACT.Relu, scale=factor)
                a[h] = a_h
                if h == 0:
                    for piece in early:
                        copy_out(piece)
            for piece in late:
                copy_out(piece)

            z5 = keep.tile([P, SC], F32, name=f"x{n % 2}", tag=f"x{n % 2}")
            v = keep.tile([P, SC], F32, name=f"x{(n + 1) % 2}", tag=f"x{(n + 1) % 2}")
            nc.gpsimd.tensor_tensor(out=v[:], in0=a[0][:], in1=a[1][:], op=ALU.add)

            z = {}
            for h in (3, 5, 7):
                z_h = z5 if h == 5 else work.tile([P, SC], F32, name=f"z{h}", tag=f"z{h}")
                nc.vector.scalar_tensor_tensor(
                    out=z_h[:], in0=banks[h][:], scalar=0.0, in1=a[h - 1][:], op0=ALU.max, op1=ALU.add
                )
                z[h] = z_h
            for piece in early:
                quantize(piece)
            if 0 < n < len(UNITS) - 1:
                store_sum(n - 1)
            for piece in late:
                quantize(piece)
            for cj in WIDENINGS.get(n, []):
                widen(cj[0], cj[1])
            s1 = work.tile([P, SC], F32, name="s1", tag="s1")
            nc.vector.scalar_tensor_tensor(
                out=s1[:], in0=z[3][:], scalar=r_sum[:, i, :], in1=z[5][:], op0=ALU.mult, op1=ALU.add
            )
            s2 = work.tile([P, SC], F32, name="s2", tag="s2")
            nc.vector.scalar_tensor_tensor(
                out=s2[:], in0=z[7][:], scalar=w_c[:, i, 7:8], in1=v[:], op0=ALU.mult, op1=ALU.add
            )
            state[n] = (s1, s2)

        for n in range(len(UNITS)):
            unit(n)
        store_sum(len(UNITS) - 2)
        store_sum(len(UNITS) - 1, parts=2)
